import numpy as np
import ml_dtypes


def mxq(x, axis, fmt="e4m3"):
    dtype, down = {"e4m3": (ml_dtypes.float8_e4m3fn, 7), "e5m2": (ml_dtypes.float8_e5m2, 14)}[fmt]
    v = np.moveaxis(np.asarray(x, np.float32).astype(ml_dtypes.bfloat16).astype(np.float64), axis, -1)
    blocks = v.reshape(v.shape[:-1] + (-1, 32))
    amax = np.abs(blocks).max(-1, keepdims=True)
    byte = np.maximum(np.where(amax > 0, np.frexp(amax)[1] - 1 + 127, 0) - down, 1)
    scale = np.exp2(byte - 127.0)
    codes = (blocks / scale).astype(np.float32).astype(dtype).astype(np.float64)
    return np.moveaxis((codes * scale).reshape(v.shape), -1, axis)


WIDE = False


def mx_kscale(k):
    if not WIDE:
        return np.ones(k)
    levels = np.array([10, -10, 5, -5, 0])
    if k % 512:
        return np.exp2(np.random.permutation(np.resize(levels, k // 32))).repeat(32)
    a = np.empty((k // 512, 16))
    for p in range(k // 512):
        a[p, :8] = np.random.permutation(np.resize(levels, 8))
        for g in range(8):
            far = levels[np.abs(levels - a[p, g]) >= 10]
            a[p, g + 8] = far[np.random.randint(len(far))]
    return np.exp2(a.ravel()).repeat(32)


def f64(x):
    return np.asarray(x).astype(np.float64)


def striped(idx):
    return np.tile(idx.reshape(-1, 16).T, (8, 1)).astype(np.uint16)


def unstriped(offs):
    return offs[:16].T.reshape(-1).astype(np.int64)


def striped8(idx):
    return np.concatenate([v.reshape(-1, 16).T for v in idx]).astype(np.uint16)


def unstriped8(offs):
    return np.stack([offs[16 * g:16 * g + 16].T.reshape(-1) for g in range(8)]).astype(np.int64)


E2M1 = np.array([0.0, 0.5, 1.0, 1.5, 2.0, 3.0, 4.0, 6.0, -0.0, -0.5, -1.0, -1.5, -2.0, -3.0, -4.0, -6.0])


def pack_weight(w, fmt):
    k, n = w.shape
    w = f64(np.asarray(w, np.float32).astype(ml_dtypes.bfloat16)).reshape(k // 32, 32, n)
    amax = np.abs(w).max(1)
    if fmt == "e4m3":
        byte = np.frexp(amax)[1] - 1 + 127 - 7
    else:
        mant, ex = np.frexp(amax / 6.0)
        byte = np.where(mant > 0.5, ex, ex - 1) + 127
    byte = np.clip(np.where(amax > 0, byte, 1), 1, 254)
    scaled = (w * np.exp2(127.0 - byte)[:, None, :]).reshape(k, n).astype(np.float32)
    by_word = np.ascontiguousarray(scaled.reshape(k // 512, 128, 4, n).transpose(0, 1, 3, 2))
    if fmt == "e4m3":
        words = by_word.astype(ml_dtypes.float8_e4m3fn).view(np.uint8)
    else:
        c = by_word.astype(ml_dtypes.float4_e2m1fn).view(np.uint8) & 0xF
        words = (c[..., 0::2] | (c[..., 1::2] << 4)).reshape(k // 512, 128, 2 * n)
    return np.ascontiguousarray(words), np.ascontiguousarray(byte.astype(np.uint8).reshape(k // 512, 16, n))


def unpack_weight(words, scales, fmt):
    g, _, n = scales.shape
    words = np.ascontiguousarray(words).reshape(g, 128, n, -1)
    if fmt == "e4m3":
        vals = words.view(ml_dtypes.float8_e4m3fn).astype(np.float64)
    else:
        nib = np.empty((g, 128, n, 4), np.uint8)
        nib[..., 0::2] = words & 0xF
        nib[..., 1::2] = words >> 4
        vals = E2M1[nib]
    vals = vals * np.repeat(np.exp2(scales.astype(np.float64) - 127.0), 8, axis=1)[..., None]
    return vals.transpose(0, 1, 3, 2).reshape(g * 512, n)


def pack_table(v):
    words, scales = pack_weight(v, "e4m3")
    return np.concatenate([words.reshape(words.shape[0], -1), scales.reshape(scales.shape[0], -1)], axis=1)


def unpack_table(tab):
    g, t = tab.shape[0], tab.shape[1] // 528
    return unpack_weight(tab[:, :512 * t].reshape(g, 128, t, 4), tab[:, 512 * t:].reshape(g, 16, t), "e4m3")


def gelu(v):
    return 0.5 * v * (1.0 + np.tanh(np.sqrt(2.0 / np.pi) * (v + 0.044715 * v**3)))


K, M, T, S = 512, 256, 4096, 2048


def setup_inputs():
    n = np.random.standard_normal
    s = mx_kscale(K)[:, None]
    return {
        "tab": pack_table(n((K, T)) * s),
        "w": (n((K, M)) / np.sqrt(K) / s).astype(np.float32),
        "b": (0.3 * n(256)).astype(np.float32),
        "wgo": np.repeat(np.random.uniform(0.5, 2.0, (8, S)), 16, axis=0).astype(np.float32),
        "offs": striped(np.random.permutation(T)[:S]),
        "offs2": striped8(np.stack([np.random.permutation(T)[:S] for _ in range(8)])),
    }


def reference(tab, w, b, wgo, offs, offs2):
    tab_ = unpack_table(tab)[:, unstriped(offs)]
    w_ = mxq(f64(w), 0, "e4m3")
    y = w_.T @ tab_
    place = unstriped8(offs2)[np.arange(M) % 128 // 16]
    out = np.zeros((M, T))
    out[np.arange(M)[:, None], place] = f64(wgo)[np.arange(M) % 128] * (gelu(y + f64(b)[:, None]))
    return out

@@ -1,0 +1,109 @@
+import concourse.mybir as mybir
+
+K, M, T, S = 512, 256, 4096, 2048
+P = 128
+FLOPS = 2 * K * M * S
+
+F32 = mybir.dt.float32
+BF16 = mybir.dt.bfloat16
+I32 = mybir.dt.int32
+U32 = mybir.dt.uint32
+U16 = mybir.dt.uint16
+U8 = mybir.dt.uint8
+FP8X4 = mybir.dt.float8_e4m3fn_x4
+COPY = mybir.ActivationFunctionType.Copy
+GELU = mybir.ActivationFunctionType.Gelu_apprx_tanh
+MULT = mybir.AluOpType.mult
+
+GATHER = 512
+SCATTER = 1024
+BANK = 512
+
+
+def tile_list_tabhs_gelu_kernel(tc, tab, w, b, wgo, offs, offs2, out):
+    nc = tc.nc
+    with (
+        tc.tile_pool(name="keep", bufs=1) as keep,
+        tc.psum_pool(name="psum", bufs=1) as psum,
+    ):
+        idx = keep.tile([P, S // 16], U16, name="idx")
+        plane = keep.tile([P, T], U8, name="plane", align_bytes=64)
+        words = keep.tile([P, T], I32, name="words", align_bytes=64)
+        nc.vector.memset(plane[:].bitcast(I32), 0)
+        nc.sync.dma_start(idx[:], offs)
+        scale_rows = tab[0, 512 * T : 528 * T].rearrange("(q t) -> q t", t=T)
+        for quad in range(4):
+            nc.sync.dma_start(
+                plane[32 * quad : 32 * quad + 4, :].bitcast(I32),
+                scale_rows[4 * quad : 4 * quad + 4, :].bitcast(I32),
+            )
+
+        zero = keep.tile([P, 1], F32, name="zero")
+        warm = keep.tile([P, 1], F32, name="warm")
+        nc.gpsimd.memset(zero[:], 0.0)
+        nc.scalar.activation(warm[:], zero[:], GELU)
+
+        nc.scalar.dma_start(words[:], tab[0, 0 : 512 * T].rearrange("(p c) -> p c", p=P).bitcast(I32))
+        w_raw = keep.tile([P, 4, M], F32, name="w_raw")
+        nc.scalar.dma_start(w_raw[:], w.rearrange("(p j) n -> p j n", j=4))
+        idx2 = keep.tile([P, S // 16], U16, name="idx2")
+        nc.sync.dma_start(idx2[:], offs2)
+        bias = keep.tile([P, 2], F32, name="bias")
+        with nc.allow_non_contiguous_dma(reason="256 values, one to a partition"):
+            nc.scalar.dma_start(bias[:], b.rearrange("(c p) -> p c", p=P))
+        factor = keep.tile([P, S], F32, name="factor")
+        for s in range(0, S, SCATTER):
+            nc.scalar.dma_start(factor[:, s : s + SCATTER], wgo[:, s : s + SCATTER])
+
+        window0 = keep.tile([P, T], F32, name="window0")
+        window1 = keep.tile([P, T], F32, name="window1")
+        windows = [window0, window1]
+        for window in windows:
+            nc.gpsimd.memset(window[:], 0.0)
+
+        w_group = keep.tile([P, M, 4], BF16, name="w_group", align_bytes=64)
+        w_codes = keep.tile([P, M], U32, name="w_codes", align_bytes=64)
+        w_scales = keep.tile([P, M], U8, name="w_scales", align_bytes=64)
+        nc.scalar.activation(w_group[:], w_raw[:].rearrange("p j n -> p n j"), COPY)
+
+        g_scales = keep.tile([P, S], U8, name="g_scales", align_bytes=64)
+        g_words = keep.tile([P, S], U32, name="g_words", align_bytes=64)
+        nc.vector.tensor_copy(g_scales[:], plane[:].indirect(idx[:]))
+
+        def gather_words(s):
+            nc.vector.tensor_copy(
+                g_words[:, s : s + GATHER],
+                words[:].bitcast(U32).indirect(idx[:, s // 16 : (s + GATHER) // 16]),
+            )
+
+        for s in (0, GATHER, 2 * GATHER):
+            gather_words(s)
+        nc.vector.quantize_mx(
+            out=w_codes[:].bitcast(FP8X4),
+            scales=w_scales[:],
+            in_=w_group[:].rearrange("p n j -> p (n j)"),
+        )
+        gather_words(3 * GATHER)
+
+        y = keep.tile([P, 2, S], F32, name="y")
+        for m in range(2):
+            for s in range(0, S, BANK):
+                bank = psum.tile([P, BANK], F32, name="bank%d_%d" % (m, s // BANK))
+                nc.tensor.matmul_mx(
+                    out=bank[:],
+                    lhsT=w_codes[:, P * m : P * m + P].bitcast(FP8X4),
+                    lhsT_scale=w_scales[:, P * m : P * m + P],
+                    rhs=g_words[:, s : s + BANK].bitcast(FP8X4),
+                    rhs_scale=g_scales[:, s : s + BANK],
+                    start=True,
+                    stop=True,
+                )
+                nc.scalar.activation(y[:, m, s : s + BANK], bank[:], GELU, bias=bias[:, m : m + 1])
+            for s in range(0, S, SCATTER):
+                nc.vector.tensor_tensor(
+                    windows[m][:].indirect(idx2[:, s // 16 : (s + SCATTER) // 16]),
+                    y[:, m, s : s + SCATTER],
+                    factor[:, s : s + SCATTER],
+                    MULT,
+                )
+            nc.sync.dma_start(out[P * m : P * m + P, :], windows[m][:])

@@ -18,6 +18,7 @@ MULT = mybir.AluOpType.mult
 GATHER = 512
 SCATTER = 1024
 BANK = 512
+CLEAR = 1024
 
 
 def tile_list_tabhs_gelu_kernel(tc, tab, w, b, wgo, offs, offs2, out):
@@ -27,39 +28,44 @@ def tile_list_tabhs_gelu_kernel(tc, tab, w, b, wgo, offs, offs2, out):
         tc.psum_pool(name="psum", bufs=1) as psum,
     ):
         idx = keep.tile([P, S // 16], U16, name="idx")
+        idx2 = keep.tile([P, S // 16], U16, name="idx2")
         plane = keep.tile([P, T], U8, name="plane", align_bytes=64)
         words = keep.tile([P, T], I32, name="words", align_bytes=64)
-        nc.vector.memset(plane[:].bitcast(I32), 0)
-        nc.sync.dma_start(idx[:], offs)
-        scale_rows = tab[0, 512 * T : 528 * T].rearrange("(q t) -> q t", t=T)
-        for quad in range(4):
-            nc.sync.dma_start(
-                plane[32 * quad : 32 * quad + 4, :].bitcast(I32),
-                scale_rows[4 * quad : 4 * quad + 4, :].bitcast(I32),
-            )
-
+        w_raw = keep.tile([P, 4, M], F32, name="w_raw")
         zero = keep.tile([P, 1], F32, name="zero")
         warm = keep.tile([P, 1], F32, name="warm")
-        nc.gpsimd.memset(zero[:], 0.0)
-        nc.scalar.activation(warm[:], zero[:], GELU)
-
-        nc.scalar.dma_start(words[:], tab[0, 0 : 512 * T].rearrange("(p c) -> p c", p=P).bitcast(I32))
-        w_raw = keep.tile([P, 4, M], F32, name="w_raw")
-        nc.scalar.dma_start(w_raw[:], w.rearrange("(p j) n -> p j n", j=4))
-        idx2 = keep.tile([P, S // 16], U16, name="idx2")
-        nc.sync.dma_start(idx2[:], offs2)
         bias = keep.tile([P, 2], F32, name="bias")
-        with nc.allow_non_contiguous_dma(reason="256 values, one to a partition"):
-            nc.scalar.dma_start(bias[:], b.rearrange("(c p) -> p c", p=P))
         factor = keep.tile([P, S], F32, name="factor")
-        for s in range(0, S, SCATTER):
-            nc.scalar.dma_start(factor[:, s : s + SCATTER], wgo[:, s : s + SCATTER])
-
         window0 = keep.tile([P, T], F32, name="window0")
         window1 = keep.tile([P, T], F32, name="window1")
         windows = [window0, window1]
-        for window in windows:
-            nc.gpsimd.memset(window[:], 0.0)
+
+        nc.gpsimd.memset(plane[:].bitcast(I32), 0)
+        nc.gpsimd.memset(zero[:], 0.0)
+        nc.scalar.dma_start(w_raw[:], w.rearrange("(p j) n -> p j n", j=4))
+        nc.sync.dma_start(idx[:], offs)
+        scale_rows = tab[0, 512 * T : 528 * T].rearrange("(q t) -> q t", t=T)
+        for quad in range(4):
+            queue = nc.sync if quad < 2 else nc.scalar
+            queue.dma_start(
+                plane[32 * quad : 32 * quad + 4, :].bitcast(I32),
+                scale_rows[4 * quad : 4 * quad + 4, :].bitcast(I32),
+            )
+        nc.scalar.activation(warm[:], zero[:], GELU)
+        nc.scalar.dma_start(words[:], tab[0, 0 : 512 * T].rearrange("(p c) -> p c", p=P).bitcast(I32))
+        nc.sync.dma_start(idx2[:], offs2)
+
+        def clear(window, first, last):
+            for c in range(first, last, CLEAR):
+                nc.gpsimd.memset(window[:, c : c + CLEAR], 0.0)
+
+        clear(window0, 0, T)
+        clear(window1, 0, T // 2)
+        with nc.allow_non_contiguous_dma(reason="256 values, one to a partition"):
+            nc.gpsimd.dma_start(bias[:], b.rearrange("(c p) -> p c", p=P))
+        for s in range(0, S, SCATTER):
+            nc.gpsimd.dma_start(factor[:, s : s + SCATTER], wgo[:, s : s + SCATTER])
+        clear(window1, T // 2, T)
 
         w_group = keep.tile([P, M, 4], BF16, name="w_group", align_bytes=64)
         w_codes = keep.tile([P, M], U32, name="w_codes", align_bytes=64)
@@ -70,20 +76,20 @@ def tile_list_tabhs_gelu_kernel(tc, tab, w, b, wgo, offs, offs2, out):
         g_words = keep.tile([P, S], U32, name="g_words", align_bytes=64)
         nc.vector.tensor_copy(g_scales[:], plane[:].indirect(idx[:]))
 
+        nc.vector.quantize_mx(
+            out=w_codes[:].bitcast(FP8X4),
+            scales=w_scales[:],
+            in_=w_group[:].rearrange("p n j -> p (n j)"),
+        )
+
         def gather_words(s):
             nc.vector.tensor_copy(
                 g_words[:, s : s + GATHER],
                 words[:].bitcast(U32).indirect(idx[:, s // 16 : (s + GATHER) // 16]),
             )
 
-        for s in (0, GATHER, 2 * GATHER):
+        for s in range(0, S, GATHER):
             gather_words(s)
-        nc.vector.quantize_mx(
-            out=w_codes[:].bitcast(FP8X4),
-            scales=w_scales[:],
-            in_=w_group[:].rearrange("p n j -> p (n j)"),
-        )
-        gather_words(3 * GATHER)
 
         y = keep.tile([P, 2, S], F32, name="y")
         for m in range(2):

@@ -15,7 +15,7 @@ COPY = mybir.ActivationFunctionType.Copy
 GELU = mybir.ActivationFunctionType.Gelu_apprx_tanh
 MULT = mybir.AluOpType.mult
 
-GATHER = 512
+GATHER = 1024
 SCATTER = 1024
 BANK = 512
 CLEAR = 1024
@@ -29,68 +29,65 @@ def tile_list_tabhs_gelu_kernel(tc, tab, w, b, wgo, offs, offs2, out):
     ):
         idx = keep.tile([P, S // 16], U16, name="idx")
         idx2 = keep.tile([P, S // 16], U16, name="idx2")
-        plane = keep.tile([P, T], U8, name="plane", align_bytes=64)
-        words = keep.tile([P, T], I32, name="words", align_bytes=64)
-        w_raw = keep.tile([P, 4, M], F32, name="w_raw")
-        zero = keep.tile([P, 1], F32, name="zero")
-        warm = keep.tile([P, 1], F32, name="warm")
-        bias = keep.tile([P, 2], F32, name="bias")
-        factor = keep.tile([P, S], F32, name="factor")
+        zero = keep.tile([P, 1], F32, tag="small", name="zero")
+        warm = keep.tile([P, 1], F32, tag="load", name="warm")
+        plane = keep.tile([P, T], U8, tag="mid", name="plane", align_bytes=64)
+        words = keep.tile([P, T], I32, tag="wide", name="words", align_bytes=64)
         window0 = keep.tile([P, T], F32, name="window0")
-        window1 = keep.tile([P, T], F32, name="window1")
-        windows = [window0, window1]
 
-        nc.gpsimd.memset(plane[:].bitcast(I32), 0)
         nc.gpsimd.memset(zero[:], 0.0)
-        nc.scalar.dma_start(w_raw[:], w.rearrange("(p j) n -> p j n", j=4))
+        nc.gpsimd.memset(plane[:].bitcast(I32), 0)
+        nc.gpsimd.memset(words[:, 0:8], 0)
         nc.sync.dma_start(idx[:], offs)
+        nc.sync.dma_start(idx2[:], offs2)
+        nc.scalar.activation(warm[:], zero[:], GELU)
         scale_rows = tab[0, 512 * T : 528 * T].rearrange("(q t) -> q t", t=T)
         for quad in range(4):
-            queue = nc.sync if quad < 2 else nc.scalar
-            queue.dma_start(
+            nc.sync.dma_start(
                 plane[32 * quad : 32 * quad + 4, :].bitcast(I32),
                 scale_rows[4 * quad : 4 * quad + 4, :].bitcast(I32),
             )
-        nc.scalar.activation(warm[:], zero[:], GELU)
-        nc.scalar.dma_start(words[:], tab[0, 0 : 512 * T].rearrange("(p c) -> p c", p=P).bitcast(I32))
-        nc.sync.dma_start(idx2[:], offs2)
-
-        def clear(window, first, last):
-            for c in range(first, last, CLEAR):
-                nc.gpsimd.memset(window[:, c : c + CLEAR], 0.0)
-
-        clear(window0, 0, T)
-        clear(window1, 0, T // 2)
+        nc.sync.dma_start(words[:], tab[0, 0 : 512 * T].rearrange("(p c) -> p c", p=P).bitcast(I32))
+        w_raw = keep.tile([P, 4, M], F32, tag="load", name="w_raw")
+        nc.sync.dma_start(w_raw[:], w.rearrange("(p j) n -> p j n", j=4))
+        bias = keep.tile([P, 2], F32, tag="small", name="bias")
         with nc.allow_non_contiguous_dma(reason="256 values, one to a partition"):
-            nc.gpsimd.dma_start(bias[:], b.rearrange("(c p) -> p c", p=P))
-        for s in range(0, S, SCATTER):
-            nc.gpsimd.dma_start(factor[:, s : s + SCATTER], wgo[:, s : s + SCATTER])
-        clear(window1, T // 2, T)
+            nc.sync.dma_start(bias[:], b.rearrange("(c p) -> p c", p=P))
+        nc.vector.memset(window0[:, 0 : T // 2], 0.0)
+        for c in range(T // 2, T, CLEAR):
+            nc.gpsimd.memset(window0[:, c : c + CLEAR], 0.0)
 
-        w_group = keep.tile([P, M, 4], BF16, name="w_group", align_bytes=64)
+        w_group = keep.tile([P, M, 4], BF16, tag="late", name="w_group", align_bytes=64)
         w_codes = keep.tile([P, M], U32, name="w_codes", align_bytes=64)
         w_scales = keep.tile([P, M], U8, name="w_scales", align_bytes=64)
         nc.scalar.activation(w_group[:], w_raw[:].rearrange("p j n -> p n j"), COPY)
 
         g_scales = keep.tile([P, S], U8, name="g_scales", align_bytes=64)
-        g_words = keep.tile([P, S], U32, name="g_words", align_bytes=64)
         nc.vector.tensor_copy(g_scales[:], plane[:].indirect(idx[:]))
+        factor = keep.tile([P, S], F32, tag="mid", name="factor", align_bytes=64)
+        for s in range(0, S, SCATTER):
+            nc.sync.dma_start(factor[:, s : s + SCATTER], wgo[:, s : s + SCATTER])
 
+        def gather_words(codes, s):
+            nc.vector.tensor_copy(
+                codes[:],
+                words[:].bitcast(U32).indirect(idx[:, s // 16 : (s + GATHER) // 16]),
+            )
+
+        codes0 = keep.tile([P, GATHER], U32, name="codes0", align_bytes=64)
+        gather_words(codes0, 0)
         nc.vector.quantize_mx(
             out=w_codes[:].bitcast(FP8X4),
             scales=w_scales[:],
             in_=w_group[:].rearrange("p n j -> p (n j)"),
         )
+        codes1 = keep.tile([P, GATHER], U32, tag="late", name="codes1", align_bytes=64)
+        gather_words(codes1, GATHER)
+        codes = [codes0, codes1]
 
-        def gather_words(s):
-            nc.vector.tensor_copy(
-                g_words[:, s : s + GATHER],
-                words[:].bitcast(U32).indirect(idx[:, s // 16 : (s + GATHER) // 16]),
-            )
-
-        for s in range(0, S, GATHER):
-            gather_words(s)
-
+        window1 = keep.tile([P, T], F32, tag="wide", name="window1", align_bytes=64)
+        nc.gpsimd.memset(window1[:], 0.0)
+        windows = [window0, window1]
         y = keep.tile([P, 2, S], F32, name="y")
         for m in range(2):
             for s in range(0, S, BANK):
@@ -99,7 +96,7 @@ def tile_list_tabhs_gelu_kernel(tc, tab, w, b, wgo, offs, offs2, out):
                     out=bank[:],
                     lhsT=w_codes[:, P * m : P * m + P].bitcast(FP8X4),
                     lhsT_scale=w_scales[:, P * m : P * m + P],
-                    rhs=g_words[:, s : s + BANK].bitcast(FP8X4),
+                    rhs=codes[s // GATHER][:, s % GATHER : s % GATHER + BANK].bitcast(FP8X4),
                     rhs_scale=g_scales[:, s : s + BANK],
                     start=True,
                     stop=True,

import concourse.mybir as mybir

K, M, T, S = 512, 256, 4096, 2048
P = 128
FLOPS = 2 * K * M * S

F32 = mybir.dt.float32
BF16 = mybir.dt.bfloat16
I32 = mybir.dt.int32
U32 = mybir.dt.uint32
U16 = mybir.dt.uint16
U8 = mybir.dt.uint8
FP8X4 = mybir.dt.float8_e4m3fn_x4
COPY = mybir.ActivationFunctionType.Copy
GELU = mybir.ActivationFunctionType.Gelu_apprx_tanh
MULT = mybir.AluOpType.mult

GATHER = 1024
SCATTER = 1024
BANK = 512
CLEAR = 1024


def tile_list_tabhs_gelu_kernel(tc, tab, w, b, wgo, offs, offs2, out):
    nc = tc.nc
    with (
        tc.tile_pool(name="keep", bufs=1) as keep,
        tc.psum_pool(name="psum", bufs=1) as psum,
    ):
        idx = keep.tile([P, S // 16], U16, name="idx")
        idx2 = keep.tile([P, S // 16], U16, name="idx2")
        zero = keep.tile([P, 1], F32, tag="small", name="zero")
        warm = keep.tile([P, 1], F32, tag="load", name="warm")
        plane = keep.tile([P, T], U8, tag="mid", name="plane", align_bytes=64)
        words = keep.tile([P, T], I32, tag="wide", name="words", align_bytes=64)
        window0 = keep.tile([P, T], F32, name="window0")

        nc.gpsimd.memset(zero[:], 0.0)
        nc.gpsimd.memset(plane[:].bitcast(I32), 0)
        nc.gpsimd.memset(words[:, 0:8], 0)
        nc.sync.dma_start(idx[:], offs)
        nc.sync.dma_start(idx2[:], offs2)
        nc.scalar.activation(warm[:], zero[:], GELU)
        scale_rows = tab[0, 512 * T : 528 * T].rearrange("(q t) -> q t", t=T)
        for quad in range(4):
            nc.sync.dma_start(
                plane[32 * quad : 32 * quad + 4, :].bitcast(I32),
                scale_rows[4 * quad : 4 * quad + 4, :].bitcast(I32),
            )
        nc.sync.dma_start(words[:], tab[0, 0 : 512 * T].rearrange("(p c) -> p c", p=P).bitcast(I32))
        w_raw = keep.tile([P, 4, M], F32, tag="load", name="w_raw")
        nc.sync.dma_start(w_raw[:], w.rearrange("(p j) n -> p j n", j=4))
        bias = keep.tile([P, 2], F32, tag="small", name="bias")
        with nc.allow_non_contiguous_dma(reason="256 values, one to a partition"):
            nc.sync.dma_start(bias[:], b.rearrange("(c p) -> p c", p=P))
        nc.vector.memset(window0[:, 0 : T // 2], 0.0)
        for c in range(T // 2, T, CLEAR):
            nc.gpsimd.memset(window0[:, c : c + CLEAR], 0.0)

        w_group = keep.tile([P, M, 4], BF16, tag="late", name="w_group", align_bytes=64)
        w_codes = keep.tile([P, M], U32, name="w_codes", align_bytes=64)
        w_scales = keep.tile([P, M], U8, name="w_scales", align_bytes=64)
        nc.scalar.activation(w_group[:], w_raw[:].rearrange("p j n -> p n j"), COPY)

        g_scales = keep.tile([P, S], U8, name="g_scales", align_bytes=64)
        nc.vector.tensor_copy(g_scales[:], plane[:].indirect(idx[:]))
        factor = keep.tile([P, S], F32, tag="mid", name="factor", align_bytes=64)
        for s in range(0, S, SCATTER):
            nc.sync.dma_start(factor[:, s : s + SCATTER], wgo[:, s : s + SCATTER])

        def gather_words(codes, s):
            nc.vector.tensor_copy(
                codes[:],
                words[:].bitcast(U32).indirect(idx[:, s // 16 : (s + GATHER) // 16]),
            )

        codes0 = keep.tile([P, GATHER], U32, name="codes0", align_bytes=64)
        gather_words(codes0, 0)
        nc.vector.quantize_mx(
            out=w_codes[:].bitcast(FP8X4),
            scales=w_scales[:],
            in_=w_group[:].rearrange("p n j -> p (n j)"),
        )
        codes1 = keep.tile([P, GATHER], U32, tag="late", name="codes1", align_bytes=64)
        gather_words(codes1, GATHER)
        codes = [codes0, codes1]

        window1 = keep.tile([P, T], F32, tag="wide", name="window1", align_bytes=64)
        nc.gpsimd.memset(window1[:], 0.0)
        windows = [window0, window1]
        y = keep.tile([P, 2, S], F32, name="y")
        for m in range(2):
            for s in range(0, S, BANK):
                bank = psum.tile([P, BANK], F32, name="bank%d_%d" % (m, s // BANK))
                nc.tensor.matmul_mx(
                    out=bank[:],
                    lhsT=w_codes[:, P * m : P * m + P].bitcast(FP8X4),
                    lhsT_scale=w_scales[:, P * m : P * m + P],
                    rhs=codes[s // GATHER][:, s % GATHER : s % GATHER + BANK].bitcast(FP8X4),
                    rhs_scale=g_scales[:, s : s + BANK],
                    start=True,
                    stop=True,
                )
                nc.scalar.activation(y[:, m, s : s + BANK], bank[:], GELU, bias=bias[:, m : m + 1])
            for s in range(0, S, SCATTER):
                nc.vector.tensor_tensor(
                    windows[m][:].indirect(idx2[:, s // 16 : (s + SCATTER) // 16]),
                    y[:, m, s : s + SCATTER],
                    factor[:, s : s + SCATTER],
                    MULT,
                )
            nc.sync.dma_start(out[P * m : P * m + P, :], windows[m][:])
